import numpy as np
import ml_dtypes


def mxq(x, axis, fmt="e4m3"):
    dtype, down = {"e4m3": (ml_dtypes.float8_e4m3fn, 7), "e5m2": (ml_dtypes.float8_e5m2, 14)}[fmt]
    v = np.moveaxis(np.asarray(x, np.float32).astype(ml_dtypes.bfloat16).astype(np.float64), axis, -1)
    blocks = v.reshape(v.shape[:-1] + (-1, 32))
    amax = np.abs(blocks).max(-1, keepdims=True)
    byte = np.maximum(np.where(amax > 0, np.frexp(amax)[1] - 1 + 127, 0) - down, 1)
    scale = np.exp2(byte - 127.0)
    codes = (blocks / scale).astype(np.float32).astype(dtype).astype(np.float64)
    return np.moveaxis((codes * scale).reshape(v.shape), -1, axis)


WIDE = False


def mx_kscale(k):
    if not WIDE:
        return np.ones(k)
    levels = np.array([10, -10, 5, -5, 0])
    if k % 512:
        return np.exp2(np.random.permutation(np.resize(levels, k // 32))).repeat(32)
    a = np.empty((k // 512, 16))
    for p in range(k // 512):
        a[p, :8] = np.random.permutation(np.resize(levels, 8))
        for g in range(8):
            far = levels[np.abs(levels - a[p, g]) >= 10]
            a[p, g + 8] = far[np.random.randint(len(far))]
    return np.exp2(a.ravel()).repeat(32)


def f64(x):
    return np.asarray(x).astype(np.float64)


def striped(idx):
    return np.tile(idx.reshape(-1, 16).T, (8, 1)).astype(np.uint16)


def unstriped(offs):
    return offs[:16].T.reshape(-1).astype(np.int64)


def striped8(idx):
    return np.concatenate([v.reshape(-1, 16).T for v in idx]).astype(np.uint16)


def unstriped8(offs):
    return np.stack([offs[16 * g:16 * g + 16].T.reshape(-1) for g in range(8)]).astype(np.int64)


E2M1 = np.array([0.0, 0.5, 1.0, 1.5, 2.0, 3.0, 4.0, 6.0, -0.0, -0.5, -1.0, -1.5, -2.0, -3.0, -4.0, -6.0])


def pack_weight(w, fmt):
    k, n = w.shape
    w = f64(np.asarray(w, np.float32).astype(ml_dtypes.bfloat16)).reshape(k // 32, 32, n)
    amax = np.abs(w).max(1)
    if fmt == "e4m3":
        byte = np.frexp(amax)[1] - 1 + 127 - 7
    else:
        mant, ex = np.frexp(amax / 6.0)
        byte = np.where(mant > 0.5, ex, ex - 1) + 127
    byte = np.clip(np.where(amax > 0, byte, 1), 1, 254)
    scaled = (w * np.exp2(127.0 - byte)[:, None, :]).reshape(k, n).astype(np.float32)
    by_word = np.ascontiguousarray(scaled.reshape(k // 512, 128, 4, n).transpose(0, 1, 3, 2))
    if fmt == "e4m3":
        words = by_word.astype(ml_dtypes.float8_e4m3fn).view(np.uint8)
    else:
        c = by_word.astype(ml_dtypes.float4_e2m1fn).view(np.uint8) & 0xF
        words = (c[..., 0::2] | (c[..., 1::2] << 4)).reshape(k // 512, 128, 2 * n)
    return np.ascontiguousarray(words), np.ascontiguousarray(byte.astype(np.uint8).reshape(k // 512, 16, n))


def unpack_weight(words, scales, fmt):
    g, _, n = scales.shape
    words = np.ascontiguousarray(words).reshape(g, 128, n, -1)
    if fmt == "e4m3":
        vals = words.view(ml_dtypes.float8_e4m3fn).astype(np.float64)
    else:
        nib = np.empty((g, 128, n, 4), np.uint8)
        nib[..., 0::2] = words & 0xF
        nib[..., 1::2] = words >> 4
        vals = E2M1[nib]
    vals = vals * np.repeat(np.exp2(scales.astype(np.float64) - 127.0), 8, axis=1)[..., None]
    return vals.transpose(0, 1, 3, 2).reshape(g * 512, n)


def pack_table(v):
    words, scales = pack_weight(v, "e4m3")
    return np.concatenate([words.reshape(words.shape[0], -1), scales.reshape(scales.shape[0], -1)], axis=1)


def unpack_table(tab):
    g, t = tab.shape[0], tab.shape[1] // 528
    return unpack_weight(tab[:, :512 * t].reshape(g, 128, t, 4), tab[:, 512 * t:].reshape(g, 16, t), "e4m3")


K, M, T, S = 1024, 512, 2048, 1024


def setup_inputs():
    n = np.random.standard_normal
    s = mx_kscale(K)[:, None]
    return {
        "tab": pack_table(n((K, T)) * s),
        "w": (n((K, M)) / np.sqrt(K) / s).astype(np.float32),
        "b": (0.3 * n(512)).astype(np.float32),
        "wgo": np.repeat(np.random.uniform(0.5, 2.0, (8, S)), 16, axis=0).astype(np.float32),
        "offs": striped(np.random.permutation(T)[:S]),
        "offs2": striped8(np.stack([np.random.permutation(T)[:S] for _ in range(8)])),
    }


def reference(tab, w, b, wgo, offs, offs2):
    tab_ = unpack_table(tab)[:, unstriped(offs)]
    w_ = mxq(f64(w), 0, "e4m3")
    y = w_.T @ tab_
    place = unstriped8(offs2)[np.arange(M) % 128 // 16]
    out = np.zeros((M, T))
    out[np.arange(M)[:, None], place] = f64(wgo)[np.arange(M) % 128] * (y + f64(b)[:, None])
    return out

@@ -1,0 +1,150 @@
+import concourse.mybir as mybir
+from concourse.masks import make_identity
+
+FLOPS = 2 * 1024 * 512 * 1024
+
+F32 = mybir.dt.float32
+BF16 = mybir.dt.bfloat16
+I32 = mybir.dt.int32
+U32 = mybir.dt.uint32
+U16 = mybir.dt.uint16
+U8 = mybir.dt.uint8
+FP8X4 = mybir.dt.float8_e4m3fn_x4
+MULT = mybir.AluOpType.mult
+ADD = mybir.AluOpType.add
+IDENTITY = mybir.ActivationFunctionType.Identity
+
+P = 128
+K, M, T, S = 1024, 512, 2048, 1024
+PASSES = K // 512
+HALF = 512
+BLOCKS = M // P
+PAIR = 2 * P
+
+
+def tile_list_tabhs_bias_kernel(tc, tab, w, b, wgo, offs, offs2, out):
+    nc = tc.nc
+    with (
+        tc.tile_pool(name="keep", bufs=1) as keep,
+        tc.tile_pool(name="ring", bufs=2) as ring,
+        tc.psum_pool(name="psum", bufs=1) as psum,
+    ):
+        pick = keep.tile([P, S // 16], U16, name="pick")
+        place = keep.tile([P, S // 16], U16, name="place")
+        nc.sync.dma_start(pick[:], offs)
+
+        scales = keep.tile([P, T], U8, name="scales", align_bytes=64)
+        nc.vector.memset(scales[:].bitcast(I32), 0)
+        scale_rows = tab[:, 512 * T :].rearrange("a (q r c) -> q a r c", q=4, r=4)
+
+        words = [keep.tile([P, T], I32, name=f"words{a}", align_bytes=64) for a in range(PASSES)]
+
+        def load_words(a):
+            nc.sync.dma_start(words[a][:], tab[a, 0 : 512 * T].rearrange("(p x) -> p x", p=P).bitcast(I32))
+
+        w_rows = w.rearrange("(a p j) m -> a p j m", a=PASSES, j=4)
+        raw = [[keep.tile([P, 4, PAIR], F32, name=f"raw{i}{a}", tag=f"raw{i}{a}") for a in range(PASSES)] for i in range(2)]
+
+        def load_weights(i, a):
+            nc.sync.dma_start(raw[i][a][:], w_rows[a][:, :, i * PAIR : (i + 1) * PAIR])
+
+        nc.sync.dma_start(place[:], offs2)
+        load_weights(0, 0)
+        for q in range(4):
+            nc.sync.dma_start(scales[32 * q : 32 * q + 8, :].bitcast(I32), scale_rows[q].bitcast(I32))
+        load_words(0)
+        load_weights(0, 1)
+        load_words(1)
+        weight = [keep.tile([P, HALF], F32, name="weight0")]
+        nc.sync.dma_start(weight[0][:], wgo[:, 0:HALF])
+        load_weights(1, 0)
+        load_weights(1, 1)
+
+        bias_rows = keep.tile([P, P], F32, name="bias_rows")
+        nc.gpsimd.memset(bias_rows[:], 0.0)
+        nc.scalar.dma_start(bias_rows[0:BLOCKS, :], b.rearrange("(c p) -> c p", p=P))
+        identity = keep.tile([P, P], F32, name="identity")
+        make_identity(nc, identity[:])
+        turned = psum.tile([P, P], F32, name="turned", tag="acc31")
+        nc.tensor.transpose(turned[:], bias_rows[:], identity[:])
+        bias = keep.tile([P, BLOCKS], F32, name="bias")
+        nc.scalar.copy(bias[:], turned[:, 0:BLOCKS])
+
+        window = [keep.tile([P, T], F32, name=f"window{m}") for m in range(BLOCKS)]
+        nc.vector.memset(window[BLOCKS - 1][:], 0.0)
+        for m in range(BLOCKS - 1):
+            nc.gpsimd.memset(window[m][:], 0.0)
+
+        picked_scales = keep.tile([P, S], U8, name="picked_scales", align_bytes=64)
+        picked0 = keep.tile([P, S], U32, name="picked0", align_bytes=64)
+        nc.vector.tensor_copy(picked_scales[:], scales[:].indirect(pick[:]))
+        nc.vector.tensor_copy(picked0[:], words[0][:].bitcast(U32).indirect(pick[:]))
+        picked1 = [keep.tile([P, HALF], U32, name=f"picked1{h}", align_bytes=64) for h in range(2)]
+
+        def codes_of(a, h):
+            return picked0[:, h * HALF : (h + 1) * HALF] if a == 0 else picked1[h][:]
+
+        grouped = {}
+
+        def interleave(i):
+            for m in (2 * i, 2 * i + 1):
+                grouped[m] = keep.tile([P, PASSES, P, 4], BF16, name=f"grouped{m}", align_bytes=64)
+            for a in range(PASSES):
+                for m in (2 * i, 2 * i + 1):
+                    c0 = (m % 2) * P
+                    nc.scalar.copy(grouped[m][:, a], raw[i][a][:, :, c0 : c0 + P].rearrange("p j c -> p c j"))
+
+        def quantize(m):
+            codes = keep.tile([P, PASSES * P], U32, name=f"codes{m}", align_bytes=64)
+            plane = keep.tile([P, PASSES * P], U8, name=f"plane{m}", align_bytes=64)
+            nc.vector.quantize_mx(out=codes[:].bitcast(FP8X4), scales=plane[:], in_=grouped[m][:].rearrange("p a c j -> p (a c j)"))
+            return codes, plane
+
+        quantized = []
+
+        def project(m, h):
+            codes, plane = quantized[m]
+            acc = psum.tile([P, HALF], F32, name=f"acc{m}{h}", tag=f"acc{m}{h}")
+            for a in range(PASSES):
+                c0 = a * P
+                nc.tensor.matmul_mx(
+                    out=acc[:],
+                    lhsT=codes[:, c0 : c0 + P].bitcast(FP8X4),
+                    lhsT_scale=plane[:, c0 : c0 + P],
+                    rhs=codes_of(a, h).bitcast(FP8X4),
+                    rhs_scale=picked_scales[4 * a : P, h * HALF : (h + 1) * HALF],
+                    start=(a == 0),
+                    stop=(a == PASSES - 1),
+                )
+            y = ring.tile([P, HALF], F32, name="y")
+            if m == 0 and h == 0:
+                nc.vector.tensor_scalar(y[:], acc[:], bias[:, m : m + 1], None, op0=ADD)
+            else:
+                nc.scalar.activation(y[:], acc[:], IDENTITY, bias=bias[:, m : m + 1])
+            return y
+
+        def put(m, h, y):
+            nc.vector.tensor_tensor(window[m][:].indirect(place[:, 32 * h : 32 * h + 32]), y[:], weight[h][:], MULT)
+
+        interleave(0)
+        quantized.append(quantize(0))
+        nc.vector.tensor_copy(picked1[0][:], words[1][:].bitcast(U32).indirect(pick[:, 0:32]))
+        y00 = project(0, 0)
+        quantized.append(quantize(1))
+        y10 = project(1, 0)
+        nc.vector.tensor_copy(picked1[1][:], words[1][:].bitcast(U32).indirect(pick[:, 32:64]))
+        put(0, 0, y00)
+        put(1, 0, y10)
+        interleave(1)
+        quantized.append(quantize(2))
+        quantized.append(quantize(3))
+        weight.append(keep.tile([P, HALF], F32, name="weight1", tag="raw10"))
+        nc.sync.dma_start(weight[1][:], wgo[:, HALF:S])
+        for m in range(2):
+            put(m, 1, project(m, 1))
+            nc.sync.dma_start(out[m * P : (m + 1) * P, :], window[m][:])
+        for h in range(2):
+            for m in range(2, BLOCKS):
+                put(m, h, project(m, h))
+        for m in range(2, BLOCKS):
+            nc.sync.dma_start(out[m * P : (m + 1) * P, :], window[m][:])

@@ -11,27 +11,27 @@ U16 = mybir.dt.uint16
 U8 = mybir.dt.uint8
 FP8X4 = mybir.dt.float8_e4m3fn_x4
 MULT = mybir.AluOpType.mult
-ADD = mybir.AluOpType.add
 IDENTITY = mybir.ActivationFunctionType.Identity
 
 P = 128
 K, M, T, S = 1024, 512, 2048, 1024
 PASSES = K // 512
-HALF = 512
+BANK = 512
+FIRST = 256
 BLOCKS = M // P
-PAIR = 2 * P
+WINDOWS = 2
 
 
 def tile_list_tabhs_bias_kernel(tc, tab, w, b, wgo, offs, offs2, out):
     nc = tc.nc
     with (
         tc.tile_pool(name="keep", bufs=1) as keep,
-        tc.tile_pool(name="ring", bufs=2) as ring,
         tc.psum_pool(name="psum", bufs=1) as psum,
     ):
         pick = keep.tile([P, S // 16], U16, name="pick")
         place = keep.tile([P, S // 16], U16, name="place")
         nc.sync.dma_start(pick[:], offs)
+        nc.sync.dma_start(place[:], offs2)
 
         scales = keep.tile([P, T], U8, name="scales", align_bytes=64)
         nc.vector.memset(scales[:].bitcast(I32), 0)
@@ -43,108 +43,101 @@ def tile_list_tabhs_bias_kernel(tc, tab, w, b, wgo, offs, offs2, out):
             nc.sync.dma_start(words[a][:], tab[a, 0 : 512 * T].rearrange("(p x) -> p x", p=P).bitcast(I32))
 
         w_rows = w.rearrange("(a p j) m -> a p j m", a=PASSES, j=4)
-        raw = [[keep.tile([P, 4, PAIR], F32, name=f"raw{i}{a}", tag=f"raw{i}{a}") for a in range(PASSES)] for i in range(2)]
+        raw = [[keep.tile([P, 4, P], F32, name=f"raw{m}{a}", tag=f"raw{m}{a}") for a in range(PASSES)] for m in range(BLOCKS)]
 
-        def load_weights(i, a):
-            nc.sync.dma_start(raw[i][a][:], w_rows[a][:, :, i * PAIR : (i + 1) * PAIR])
+        def load_weights(m):
+            for a in range(PASSES):
+                nc.sync.dma_start(raw[m][a][:], w_rows[a][:, :, m * P : (m + 1) * P])
 
-        nc.sync.dma_start(place[:], offs2)
-        load_weights(0, 0)
+        gate_first = keep.tile([P, FIRST], F32, name="gate_first")
+        gate = keep.tile([P, S], F32, name="gate")
+
         for q in range(4):
             nc.sync.dma_start(scales[32 * q : 32 * q + 8, :].bitcast(I32), scale_rows[q].bitcast(I32))
         load_words(0)
-        load_weights(0, 1)
+        load_weights(0)
         load_words(1)
-        weight = [keep.tile([P, HALF], F32, name="weight0")]
-        nc.sync.dma_start(weight[0][:], wgo[:, 0:HALF])
-        load_weights(1, 0)
-        load_weights(1, 1)
+        nc.sync.dma_start(gate_first[:], wgo[:, 0:FIRST])
+        load_weights(1)
+        nc.sync.dma_start(gate[:], wgo)
+        load_weights(2)
+        load_weights(3)
 
         bias_rows = keep.tile([P, P], F32, name="bias_rows")
         nc.gpsimd.memset(bias_rows[:], 0.0)
         nc.scalar.dma_start(bias_rows[0:BLOCKS, :], b.rearrange("(c p) -> c p", p=P))
         identity = keep.tile([P, P], F32, name="identity")
         make_identity(nc, identity[:])
-        turned = psum.tile([P, P], F32, name="turned", tag="acc31")
+        turned = psum.tile([P, P], F32, name="turned", tag="bank7")
         nc.tensor.transpose(turned[:], bias_rows[:], identity[:])
         bias = keep.tile([P, BLOCKS], F32, name="bias")
         nc.scalar.copy(bias[:], turned[:, 0:BLOCKS])
 
-        window = [keep.tile([P, T], F32, name=f"window{m}") for m in range(BLOCKS)]
-        nc.vector.memset(window[BLOCKS - 1][:], 0.0)
-        for m in range(BLOCKS - 1):
-            nc.gpsimd.memset(window[m][:], 0.0)
+        window = [keep.tile([P, T], F32, name=f"window{i}") for i in range(WINDOWS)]
+        nc.vector.memset(window[0][:], 0.0)
+        for i in range(1, WINDOWS):
+            nc.gpsimd.memset(window[i][:], 0.0)
 
         picked_scales = keep.tile([P, S], U8, name="picked_scales", align_bytes=64)
-        picked0 = keep.tile([P, S], U32, name="picked0", align_bytes=64)
+        picked = [keep.tile([P, S], U32, name=f"picked{a}", align_bytes=64) for a in range(PASSES)]
+
+        def gather_words(a, lo, hi):
+            nc.vector.tensor_copy(picked[a][:, lo:hi], words[a][:].bitcast(U32).indirect(pick[:, lo // 16 : hi // 16]))
+
         nc.vector.tensor_copy(picked_scales[:], scales[:].indirect(pick[:]))
-        nc.vector.tensor_copy(picked0[:], words[0][:].bitcast(U32).indirect(pick[:]))
-        picked1 = [keep.tile([P, HALF], U32, name=f"picked1{h}", align_bytes=64) for h in range(2)]
-
-        def codes_of(a, h):
-            return picked0[:, h * HALF : (h + 1) * HALF] if a == 0 else picked1[h][:]
-
-        grouped = {}
-
-        def interleave(i):
-            for m in (2 * i, 2 * i + 1):
-                grouped[m] = keep.tile([P, PASSES, P, 4], BF16, name=f"grouped{m}", align_bytes=64)
-            for a in range(PASSES):
-                for m in (2 * i, 2 * i + 1):
-                    c0 = (m % 2) * P
-                    nc.scalar.copy(grouped[m][:, a], raw[i][a][:, :, c0 : c0 + P].rearrange("p j c -> p c j"))
+        gather_words(0, 0, S)
 
         def quantize(m):
+            grouped = keep.tile([P, PASSES, P, 4], BF16, name=f"grouped{m}", align_bytes=64)
+            for a in range(PASSES):
+                nc.scalar.copy(grouped[:, a], raw[m][a][:].rearrange("p j c -> p c j"))
             codes = keep.tile([P, PASSES * P], U32, name=f"codes{m}", align_bytes=64)
             plane = keep.tile([P, PASSES * P], U8, name=f"plane{m}", align_bytes=64)
-            nc.vector.quantize_mx(out=codes[:].bitcast(FP8X4), scales=plane[:], in_=grouped[m][:].rearrange("p a c j -> p (a c j)"))
+            nc.vector.quantize_mx(out=codes[:].bitcast(FP8X4), scales=plane[:], in_=grouped[:].rearrange("p a c j -> p (a c j)"))
             return codes, plane
 
-        quantized = []
-
-        def project(m, h):
-            codes, plane = quantized[m]
-            acc = psum.tile([P, HALF], F32, name=f"acc{m}{h}", tag=f"acc{m}{h}")
+        def project(m, quantized, lo, hi, bank, y):
+            codes, plane = quantized
+            acc = psum.tile([P, hi - lo], F32, name=f"acc{m}_{lo}", tag=f"bank{bank}")
             for a in range(PASSES):
                 c0 = a * P
                 nc.tensor.matmul_mx(
                     out=acc[:],
                     lhsT=codes[:, c0 : c0 + P].bitcast(FP8X4),
                     lhsT_scale=plane[:, c0 : c0 + P],
-                    rhs=codes_of(a, h).bitcast(FP8X4),
-                    rhs_scale=picked_scales[4 * a : P, h * HALF : (h + 1) * HALF],
+                    rhs=picked[a][:, lo:hi].bitcast(FP8X4),
+                    rhs_scale=picked_scales[4 * a : P, lo:hi],
                     start=(a == 0),
                     stop=(a == PASSES - 1),
                 )
-            y = ring.tile([P, HALF], F32, name="y")
-            if m == 0 and h == 0:
-                nc.vector.tensor_scalar(y[:], acc[:], bias[:, m : m + 1], None, op0=ADD)
+            nc.scalar.activation(y, acc[:], IDENTITY, bias=bias[:, m : m + 1])
+
+        def put(m, lo, hi, y, weights):
+            nc.vector.tensor_tensor(window[m % WINDOWS][:].indirect(place[:, lo // 16 : hi // 16]), y, weights, MULT)
+
+        def store(m):
+            nc.sync.dma_start(out[m * P : (m + 1) * P, :], window[m % WINDOWS][:])
+
+        quantized = quantize(0)
+        gather_words(1, 0, FIRST)
+        gather_words(1, FIRST, S)
+        y_first = keep.tile([P, FIRST], F32, name="y_first")
+        project(0, quantized, 0, FIRST, 0, y_first[:])
+        put(0, 0, FIRST, y_first[:], gate_first[:])
+        following = quantize(1)
+        y_rest = keep.tile([P, S - FIRST], F32, name="y_rest", tag="raw11")
+        project(0, quantized, FIRST, BANK, 1, y_rest[:, 0 : BANK - FIRST])
+        project(0, quantized, BANK, S, 2, y_rest[:, BANK - FIRST : S - FIRST])
+        put(0, FIRST, S, y_rest[:], gate[:, FIRST:S])
+        store(0)
+        for m in range(1, BLOCKS):
+            quantized = following
+            if m + 1 < BLOCKS:
+                following = quantize(m + 1)
+                y = keep.tile([P, S], F32, name=f"y{m}", tag=f"raw{m + 1}1")
             else:
-                nc.scalar.activation(y[:], acc[:], IDENTITY, bias=bias[:, m : m + 1])
-            return y
-
-        def put(m, h, y):
-            nc.vector.tensor_tensor(window[m][:].indirect(place[:, 32 * h : 32 * h + 32]), y[:], weight[h][:], MULT)
-
-        interleave(0)
-        quantized.append(quantize(0))
-        nc.vector.tensor_copy(picked1[0][:], words[1][:].bitcast(U32).indirect(pick[:, 0:32]))
-        y00 = project(0, 0)
-        quantized.append(quantize(1))
-        y10 = project(1, 0)
-        nc.vector.tensor_copy(picked1[1][:], words[1][:].bitcast(U32).indirect(pick[:, 32:64]))
-        put(0, 0, y00)
-        put(1, 0, y10)
-        interleave(1)
-        quantized.append(quantize(2))
-        quantized.append(quantize(3))
-        weight.append(keep.tile([P, HALF], F32, name="weight1", tag="raw10"))
-        nc.sync.dma_start(weight[1][:], wgo[:, HALF:S])
-        for m in range(2):
-            put(m, 1, project(m, 1))
-            nc.sync.dma_start(out[m * P : (m + 1) * P, :], window[m][:])
-        for h in range(2):
-            for m in range(2, BLOCKS):
-                put(m, h, project(m, h))
-        for m in range(2, BLOCKS):
-            nc.sync.dma_start(out[m * P : (m + 1) * P, :], window[m][:])
+                y = keep.tile([P, S], F32, name=f"y{m}")
+            for h in range(S // BANK):
+                project(m, quantized, h * BANK, (h + 1) * BANK, (1 + 2 * m + h) % 8, y[:, h * BANK : (h + 1) * BANK])
+            put(m, 0, S, y[:], gate[:])
+            store(m)

@@ -31,7 +31,6 @@ def tile_list_tabhs_bias_kernel(tc, tab, w, b, wgo, offs, offs2, out):
         pick = keep.tile([P, S // 16], U16, name="pick")
         place = keep.tile([P, S // 16], U16, name="place")
         nc.sync.dma_start(pick[:], offs)
-        nc.sync.dma_start(place[:], offs2)
 
         scales = keep.tile([P, T], U8, name="scales", align_bytes=64)
         nc.vector.memset(scales[:].bitcast(I32), 0)
@@ -52,11 +51,12 @@ def tile_list_tabhs_bias_kernel(tc, tab, w, b, wgo, offs, offs2, out):
         gate_first = keep.tile([P, FIRST], F32, name="gate_first")
         gate = keep.tile([P, S], F32, name="gate")
 
+        load_words(0)
         for q in range(4):
             nc.sync.dma_start(scales[32 * q : 32 * q + 8, :].bitcast(I32), scale_rows[q].bitcast(I32))
-        load_words(0)
         load_weights(0)
         load_words(1)
+        nc.sync.dma_start(place[:], offs2)
         nc.sync.dma_start(gate_first[:], wgo[:, 0:FIRST])
         load_weights(1)
         nc.sync.dma_start(gate[:], wgo)
@@ -84,8 +84,8 @@ def tile_list_tabhs_bias_kernel(tc, tab, w, b, wgo, offs, offs2, out):
         def gather_words(a, lo, hi):
             nc.vector.tensor_copy(picked[a][:, lo:hi], words[a][:].bitcast(U32).indirect(pick[:, lo // 16 : hi // 16]))
 
-        nc.vector.tensor_copy(picked_scales[:], scales[:].indirect(pick[:]))
         gather_words(0, 0, S)
+        nc.vector.tensor_copy(picked_scales[:], scales[:].indirect(pick[:]))
 
         def quantize(m):
             grouped = keep.tile([P, PASSES, P, 4], BF16, name=f"grouped{m}", align_bytes=64)

@@ -73,10 +73,8 @@ def tile_list_tabhs_bias_kernel(tc, tab, w, b, wgo, offs, offs2, out):
         bias = keep.tile([P, BLOCKS], F32, name="bias")
         nc.scalar.copy(bias[:], turned[:, 0:BLOCKS])
 
-        window = [keep.tile([P, T], F32, name=f"window{i}") for i in range(WINDOWS)]
+        window = [keep.tile([P, T], F32, name="window0")]
         nc.vector.memset(window[0][:], 0.0)
-        for i in range(1, WINDOWS):
-            nc.gpsimd.memset(window[i][:], 0.0)
 
         picked_scales = keep.tile([P, S], U8, name="picked_scales", align_bytes=64)
         picked = [keep.tile([P, S], U32, name=f"picked{a}", align_bytes=64) for a in range(PASSES)]
@@ -88,7 +86,7 @@ def tile_list_tabhs_bias_kernel(tc, tab, w, b, wgo, offs, offs2, out):
         nc.vector.tensor_copy(picked_scales[:], scales[:].indirect(pick[:]))
 
         def quantize(m):
-            grouped = keep.tile([P, PASSES, P, 4], BF16, name=f"grouped{m}", align_bytes=64)
+            grouped = keep.tile([P, PASSES, P, 4], BF16, name=f"grouped{m}", tag=f"grouped{m}", align_bytes=64)
             for a in range(PASSES):
                 nc.scalar.copy(grouped[:, a], raw[m][a][:].rearrange("p j c -> p c j"))
             codes = keep.tile([P, PASSES * P], U32, name=f"codes{m}", align_bytes=64)
@@ -125,6 +123,8 @@ def tile_list_tabhs_bias_kernel(tc, tab, w, b, wgo, offs, offs2, out):
         project(0, quantized, 0, FIRST, 0, y_first[:])
         put(0, 0, FIRST, y_first[:], gate_first[:])
         following = quantize(1)
+        window.append(keep.tile([P, T], F32, name="window1", tag="grouped1", align_bytes=64))
+        nc.gpsimd.memset(window[1][:], 0.0)
         y_rest = keep.tile([P, S - FIRST], F32, name="y_rest", tag="raw11")
         project(0, quantized, FIRST, BANK, 1, y_rest[:, 0 : BANK - FIRST])
         project(0, quantized, BANK, S, 2, y_rest[:, BANK - FIRST : S - FIRST])

@@ -48,7 +48,6 @@ def tile_list_tabhs_bias_kernel(tc, tab, w, b, wgo, offs, offs2, out):
             for a in range(PASSES):
                 nc.sync.dma_start(raw[m][a][:], w_rows[a][:, :, m * P : (m + 1) * P])
 
-        gate_first = keep.tile([P, FIRST], F32, name="gate_first")
         gate = keep.tile([P, S], F32, name="gate")
 
         load_words(0)
@@ -57,9 +56,9 @@ def tile_list_tabhs_bias_kernel(tc, tab, w, b, wgo, offs, offs2, out):
         load_weights(0)
         load_words(1)
         nc.sync.dma_start(place[:], offs2)
-        nc.sync.dma_start(gate_first[:], wgo[:, 0:FIRST])
+        nc.sync.dma_start(gate[:, 0:FIRST], wgo[:, 0:FIRST])
         load_weights(1)
-        nc.sync.dma_start(gate[:], wgo)
+        nc.sync.dma_start(gate[:, FIRST:S], wgo[:, FIRST:S])
         load_weights(2)
         load_weights(3)
 
@@ -74,7 +73,7 @@ def tile_list_tabhs_bias_kernel(tc, tab, w, b, wgo, offs, offs2, out):
         nc.scalar.copy(bias[:], turned[:, 0:BLOCKS])
 
         window = [keep.tile([P, T], F32, name="window0")]
-        nc.vector.memset(window[0][:], 0.0)
+        nc.gpsimd.memset(window[0][:], 0.0)
 
         picked_scales = keep.tile([P, S], U8, name="picked_scales", align_bytes=64)
         picked = [keep.tile([P, S], U32, name=f"picked{a}", align_bytes=64) for a in range(PASSES)]
@@ -121,7 +120,7 @@ def tile_list_tabhs_bias_kernel(tc, tab, w, b, wgo, offs, offs2, out):
         gather_words(1, FIRST, S)
         y_first = keep.tile([P, FIRST], F32, name="y_first")
         project(0, quantized, 0, FIRST, 0, y_first[:])
-        put(0, 0, FIRST, y_first[:], gate_first[:])
+        put(0, 0, FIRST, y_first[:], gate[:, 0:FIRST])
         following = quantize(1)
         window.append(keep.tile([P, T], F32, name="window1", tag="grouped1", align_bytes=64))
         nc.gpsimd.memset(window[1][:], 0.0)

@@ -73,7 +73,7 @@ def tile_list_tabhs_bias_kernel(tc, tab, w, b, wgo, offs, offs2, out):
         nc.scalar.copy(bias[:], turned[:, 0:BLOCKS])
 
         window = [keep.tile([P, T], F32, name="window0")]
-        nc.gpsimd.memset(window[0][:], 0.0)
+        nc.vector.memset(window[0][:], 0.0)
 
         picked_scales = keep.tile([P, S], U8, name="picked_scales", align_bytes=64)
         picked = [keep.tile([P, S], U32, name=f"picked{a}", align_bytes=64) for a in range(PASSES)]
@@ -113,7 +113,12 @@ def tile_list_tabhs_bias_kernel(tc, tab, w, b, wgo, offs, offs2, out):
             nc.vector.tensor_tensor(window[m % WINDOWS][:].indirect(place[:, lo // 16 : hi // 16]), y, weights, MULT)
 
         def store(m):
-            nc.sync.dma_start(out[m * P : (m + 1) * P, :], window[m % WINDOWS][:])
+            rows = out[m * P : (m + 1) * P, :]
+            if m + 1 < BLOCKS:
+                nc.sync.dma_start(rows, window[m % WINDOWS][:])
+            else:
+                nc.sync.dma_start(rows[:, 0 : T // 2], window[m % WINDOWS][:, 0 : T // 2])
+                nc.scalar.dma_start(rows[:, T // 2 : T], window[m % WINDOWS][:, T // 2 : T])
 
         quantized = quantize(0)
         gather_words(1, 0, FIRST)

@@ -30,7 +30,6 @@ def tile_list_tabhs_bias_kernel(tc, tab, w, b, wgo, offs, offs2, out):
     ):
         pick = keep.tile([P, S // 16], U16, name="pick")
         place = keep.tile([P, S // 16], U16, name="place")
-        nc.sync.dma_start(pick[:], offs)
 
         scales = keep.tile([P, T], U8, name="scales", align_bytes=64)
         nc.vector.memset(scales[:].bitcast(I32), 0)
@@ -51,6 +50,7 @@ def tile_list_tabhs_bias_kernel(tc, tab, w, b, wgo, offs, offs2, out):
         gate = keep.tile([P, S], F32, name="gate")
 
         load_words(0)
+        nc.sync.dma_start(pick[:], offs)
         for q in range(4):
             nc.sync.dma_start(scales[32 * q : 32 * q + 8, :].bitcast(I32), scale_rows[q].bitcast(I32))
         load_weights(0)
@@ -87,7 +87,10 @@ def tile_list_tabhs_bias_kernel(tc, tab, w, b, wgo, offs, offs2, out):
         def quantize(m):
             grouped = keep.tile([P, PASSES, P, 4], BF16, name=f"grouped{m}", tag=f"grouped{m}", align_bytes=64)
             for a in range(PASSES):
-                nc.scalar.copy(grouped[:, a], raw[m][a][:].rearrange("p j c -> p c j"))
+                nc.scalar.copy(
+                    grouped[:, a].rearrange("p (c i) j -> p c j i", i=4),
+                    raw[m][a][:].rearrange("p j (c i) -> p c j i", i=4),
+                )
             codes = keep.tile([P, PASSES * P], U32, name=f"codes{m}", align_bytes=64)
             plane = keep.tile([P, PASSES * P], U8, name=f"plane{m}", align_bytes=64)
             nc.vector.quantize_mx(out=codes[:].bitcast(FP8X4), scales=plane[:], in_=grouped[:].rearrange("p a c j -> p (a c j)"))

@@ -31,36 +31,38 @@ def tile_list_tabhs_bias_kernel(tc, tab, w, b, wgo, offs, offs2, out):
         pick = keep.tile([P, S // 16], U16, name="pick")
         place = keep.tile([P, S // 16], U16, name="place")
 
-        scales = keep.tile([P, T], U8, name="scales", align_bytes=64)
+        scales = keep.tile([P, T], U8, name="scales", tag="picked0", align_bytes=64)
         nc.vector.memset(scales[:].bitcast(I32), 0)
-        scale_rows = tab[:, 512 * T :].rearrange("a (q r c) -> q a r c", q=4, r=4)
+        scale_rows = tab[:, 512 * T :].rearrange("a (i c) -> i a c", i=16)
+        planes = keep.tile([P, PASSES * S], U8, name="planes", align_bytes=64)
+        nc.vector.memset(planes[:].bitcast(I32), 0)
+        warm = keep.tile([P, 2], F32, name="warm")
+        nc.vector.memset(warm[:, 0:1], 0.0)
 
-        words = [keep.tile([P, T], I32, name=f"words{a}", align_bytes=64) for a in range(PASSES)]
+        words = [keep.tile([P, T], I32, name=f"words{a}", tag=f"words{a}", align_bytes=64) for a in range(PASSES)]
 
         def load_words(a):
             nc.sync.dma_start(words[a][:], tab[a, 0 : 512 * T].rearrange("(p x) -> p x", p=P).bitcast(I32))
 
         w_rows = w.rearrange("(a p j) m -> a p j m", a=PASSES, j=4)
-        raw = [[keep.tile([P, 4, P], F32, name=f"raw{m}{a}", tag=f"raw{m}{a}") for a in range(PASSES)] for m in range(BLOCKS)]
+        slot = [["slot00", "slot01"], ["slot10", "slot00"], ["slot01", "grouped0"], ["slot10", "slot01"]]
+        raw = {}
 
         def load_weights(m):
             for a in range(PASSES):
-                nc.sync.dma_start(raw[m][a][:], w_rows[a][:, :, m * P : (m + 1) * P])
+                raw[m, a] = keep.tile([P, 4, P], F32, name=f"raw{m}{a}", tag=slot[m][a], align_bytes=64)
+                nc.sync.dma_start(raw[m, a][:], w_rows[a][:, :, m * P : (m + 1) * P])
 
         gate = keep.tile([P, S], F32, name="gate")
 
-        load_words(0)
         nc.sync.dma_start(pick[:], offs)
-        for q in range(4):
-            nc.sync.dma_start(scales[32 * q : 32 * q + 8, :].bitcast(I32), scale_rows[q].bitcast(I32))
+        load_words(0)
+        nc.scalar.dma_start(scales[0:P:4, :].bitcast(I32), scale_rows.bitcast(I32))
+        nc.scalar.activation(warm[:, 1:2], warm[:, 0:1], IDENTITY)
+        nc.sync.dma_start(place[:], offs2)
         load_weights(0)
         load_words(1)
-        nc.sync.dma_start(place[:], offs2)
-        nc.sync.dma_start(gate[:, 0:FIRST], wgo[:, 0:FIRST])
-        load_weights(1)
-        nc.sync.dma_start(gate[:, FIRST:S], wgo[:, FIRST:S])
-        load_weights(2)
-        load_weights(3)
+        nc.sync.dma_start(gate[:], wgo)
 
         bias_rows = keep.tile([P, P], F32, name="bias_rows")
         nc.gpsimd.memset(bias_rows[:], 0.0)
@@ -73,25 +75,29 @@ def tile_list_tabhs_bias_kernel(tc, tab, w, b, wgo, offs, offs2, out):
         nc.scalar.copy(bias[:], turned[:, 0:BLOCKS])
 
         window = [keep.tile([P, T], F32, name="window0")]
-        nc.vector.memset(window[0][:], 0.0)
+        nc.gpsimd.memset(window[0][:], 0.0)
 
-        picked_scales = keep.tile([P, S], U8, name="picked_scales", align_bytes=64)
-        picked = [keep.tile([P, S], U32, name=f"picked{a}", align_bytes=64) for a in range(PASSES)]
+        picked_scales = keep.tile([P, S], U8, name="picked_scales", tag="slot10", align_bytes=64)
 
         def gather_words(a, lo, hi):
             nc.vector.tensor_copy(picked[a][:, lo:hi], words[a][:].bitcast(U32).indirect(pick[:, lo // 16 : hi // 16]))
 
-        gather_words(0, 0, S)
         nc.vector.tensor_copy(picked_scales[:], scales[:].indirect(pick[:]))
+        for q in range(4):
+            nc.scalar.dma_start(
+                planes[32 * q : 32 * q + 4, :].bitcast(I32), picked_scales[32 * q : 32 * q + 32 : 4, :].bitcast(I32)
+            )
+        picked = [keep.tile([P, S], U32, name=f"picked{a}", tag=f"picked{a}", align_bytes=64) for a in range(PASSES)]
+        gather_words(0, 0, S)
 
         def quantize(m):
             grouped = keep.tile([P, PASSES, P, 4], BF16, name=f"grouped{m}", tag=f"grouped{m}", align_bytes=64)
             for a in range(PASSES):
                 nc.scalar.copy(
                     grouped[:, a].rearrange("p (c i) j -> p c j i", i=4),
-                    raw[m][a][:].rearrange("p j (c i) -> p c j i", i=4),
+                    raw[m, a][:].rearrange("p j (c i) -> p c j i", i=4),
                 )
-            codes = keep.tile([P, PASSES * P], U32, name=f"codes{m}", align_bytes=64)
+            codes = keep.tile([P, PASSES * P], U32, name=f"codes{m}", tag="words0" if m == 0 else f"codes{m}", align_bytes=64)
             plane = keep.tile([P, PASSES * P], U8, name=f"plane{m}", align_bytes=64)
             nc.vector.quantize_mx(out=codes[:].bitcast(FP8X4), scales=plane[:], in_=grouped[:].rearrange("p a c j -> p (a c j)"))
             return codes, plane
@@ -106,7 +112,7 @@ def tile_list_tabhs_bias_kernel(tc, tab, w, b, wgo, offs, offs2, out):
                     lhsT=codes[:, c0 : c0 + P].bitcast(FP8X4),
                     lhsT_scale=plane[:, c0 : c0 + P],
                     rhs=picked[a][:, lo:hi].bitcast(FP8X4),
-                    rhs_scale=picked_scales[4 * a : P, lo:hi],
+                    rhs_scale=planes[:, a * S + lo : a * S + hi],
                     start=(a == 0),
                     stop=(a == PASSES - 1),
                 )
@@ -124,15 +130,17 @@ def tile_list_tabhs_bias_kernel(tc, tab, w, b, wgo, offs, offs2, out):
                 nc.scalar.dma_start(rows[:, T // 2 : T], window[m % WINDOWS][:, T // 2 : T])
 
         quantized = quantize(0)
+        load_weights(1)
         gather_words(1, 0, FIRST)
         gather_words(1, FIRST, S)
         y_first = keep.tile([P, FIRST], F32, name="y_first")
         project(0, quantized, 0, FIRST, 0, y_first[:])
         put(0, 0, FIRST, y_first[:], gate[:, 0:FIRST])
         following = quantize(1)
+        load_weights(2)
         window.append(keep.tile([P, T], F32, name="window1", tag="grouped1", align_bytes=64))
         nc.gpsimd.memset(window[1][:], 0.0)
-        y_rest = keep.tile([P, S - FIRST], F32, name="y_rest", tag="raw11")
+        y_rest = keep.tile([P, S - FIRST], F32, name="y_rest", tag=slot[1][1], align_bytes=64)
         project(0, quantized, FIRST, BANK, 1, y_rest[:, 0 : BANK - FIRST])
         project(0, quantized, BANK, S, 2, y_rest[:, BANK - FIRST : S - FIRST])
         put(0, FIRST, S, y_rest[:], gate[:, FIRST:S])
@@ -141,7 +149,9 @@ def tile_list_tabhs_bias_kernel(tc, tab, w, b, wgo, offs, offs2, out):
             quantized = following
             if m + 1 < BLOCKS:
                 following = quantize(m + 1)
-                y = keep.tile([P, S], F32, name=f"y{m}", tag=f"raw{m + 1}1")
+                if m + 2 < BLOCKS:
+                    load_weights(m + 2)
+                y = keep.tile([P, S], F32, name=f"y{m}", tag=slot[m + 1][1], align_bytes=64)
             else:
                 y = keep.tile([P, S], F32, name=f"y{m}")
             for h in range(S // BANK):

@@ -26,6 +26,7 @@ def tile_list_tabhs_bias_kernel(tc, tab, w, b, wgo, offs, offs2, out):
     nc = tc.nc
     with (
         tc.tile_pool(name="keep", bufs=1) as keep,
+        tc.tile_pool(name="reuse", bufs=1) as reuse,
         tc.psum_pool(name="psum", bufs=1) as psum,
     ):
         pick = keep.tile([P, S // 16], U16, name="pick")
@@ -34,23 +35,28 @@ def tile_list_tabhs_bias_kernel(tc, tab, w, b, wgo, offs, offs2, out):
         scales = keep.tile([P, T], U8, name="scales", tag="picked0", align_bytes=64)
         nc.vector.memset(scales[:].bitcast(I32), 0)
         scale_rows = tab[:, 512 * T :].rearrange("a (i c) -> i a c", i=16)
+        bias_rows = keep.tile([P, P], F32, name="bias_rows")
+        nc.vector.memset(bias_rows[:], 0.0)
         planes = keep.tile([P, PASSES * S], U8, name="planes", align_bytes=64)
         nc.vector.memset(planes[:].bitcast(I32), 0)
         warm = keep.tile([P, 2], F32, name="warm")
         nc.vector.memset(warm[:, 0:1], 0.0)
 
-        words = [keep.tile([P, T], I32, name=f"words{a}", tag=f"words{a}", align_bytes=64) for a in range(PASSES)]
+        words = [reuse.tile([P, T], I32, name="words0", offset=0), keep.tile([P, T], I32, name="words1", align_bytes=64)]
 
         def load_words(a):
             nc.sync.dma_start(words[a][:], tab[a, 0 : 512 * T].rearrange("(p x) -> p x", p=P).bitcast(I32))
 
         w_rows = w.rearrange("(a p j) m -> a p j m", a=PASSES, j=4)
-        slot = [["slot00", "slot01"], ["slot10", "slot00"], ["slot01", "grouped0"], ["slot10", "slot01"]]
+        start = {(1, 0): 1024, (1, 1): 5120, (2, 0): 3072, (3, 0): 1024, (3, 1): 3072}
         raw = {}
 
         def load_weights(m):
             for a in range(PASSES):
-                raw[m, a] = keep.tile([P, 4, P], F32, name=f"raw{m}{a}", tag=slot[m][a], align_bytes=64)
+                if (m, a) in start:
+                    raw[m, a] = reuse.tile([P, 4, P], F32, name=f"raw{m}{a}", offset=start[m, a])
+                else:
+                    raw[m, a] = keep.tile([P, 4, P], F32, name=f"raw{m}{a}", tag="grouped0" if m else f"raw{m}{a}", align_bytes=64)
                 nc.sync.dma_start(raw[m, a][:], w_rows[a][:, :, m * P : (m + 1) * P])
 
         gate = keep.tile([P, S], F32, name="gate")
@@ -58,26 +64,26 @@ def tile_list_tabhs_bias_kernel(tc, tab, w, b, wgo, offs, offs2, out):
         nc.sync.dma_start(pick[:], offs)
         load_words(0)
         nc.scalar.dma_start(scales[0:P:4, :].bitcast(I32), scale_rows.bitcast(I32))
+        nc.scalar.dma_start(bias_rows[0:BLOCKS, :], b.rearrange("(c p) -> c p", p=P))
         nc.scalar.activation(warm[:, 1:2], warm[:, 0:1], IDENTITY)
         nc.sync.dma_start(place[:], offs2)
         load_weights(0)
         load_words(1)
         nc.sync.dma_start(gate[:], wgo)
 
-        bias_rows = keep.tile([P, P], F32, name="bias_rows")
-        nc.gpsimd.memset(bias_rows[:], 0.0)
-        nc.scalar.dma_start(bias_rows[0:BLOCKS, :], b.rearrange("(c p) -> c p", p=P))
         identity = keep.tile([P, P], F32, name="identity")
         make_identity(nc, identity[:])
         turned = psum.tile([P, P], F32, name="turned", tag="bank7")
         nc.tensor.transpose(turned[:], bias_rows[:], identity[:])
         bias = keep.tile([P, BLOCKS], F32, name="bias")
         nc.scalar.copy(bias[:], turned[:, 0:BLOCKS])
+        bias_first = keep.tile([P, 1], F32, name="bias_first", tag="grouped1", align_bytes=64)
+        nc.scalar.copy(bias_first[:], turned[:, 0:1])
 
         window = [keep.tile([P, T], F32, name="window0")]
         nc.gpsimd.memset(window[0][:], 0.0)
 
-        picked_scales = keep.tile([P, S], U8, name="picked_scales", tag="slot10", align_bytes=64)
+        picked_scales = keep.tile([P, S], U8, name="picked_scales", align_bytes=64)
 
         def gather_words(a, lo, hi):
             nc.vector.tensor_copy(picked[a][:, lo:hi], words[a][:].bitcast(U32).indirect(pick[:, lo // 16 : hi // 16]))
@@ -97,12 +103,15 @@ def tile_list_tabhs_bias_kernel(tc, tab, w, b, wgo, offs, offs2, out):
                     grouped[:, a].rearrange("p (c i) j -> p c j i", i=4),
                     raw[m, a][:].rearrange("p j (c i) -> p c j i", i=4),
                 )
-            codes = keep.tile([P, PASSES * P], U32, name=f"codes{m}", tag="words0" if m == 0 else f"codes{m}", align_bytes=64)
+            if m == 0:
+                codes = reuse.tile([P, PASSES * P], U32, name="codes0", offset=0, align_bytes=64)
+            else:
+                codes = keep.tile([P, PASSES * P], U32, name=f"codes{m}", align_bytes=64)
             plane = keep.tile([P, PASSES * P], U8, name=f"plane{m}", align_bytes=64)
             nc.vector.quantize_mx(out=codes[:].bitcast(FP8X4), scales=plane[:], in_=grouped[:].rearrange("p a c j -> p (a c j)"))
             return codes, plane
 
-        def project(m, quantized, lo, hi, bank, y):
+        def project(m, quantized, lo, hi, bank, y, column):
             codes, plane = quantized
             acc = psum.tile([P, hi - lo], F32, name=f"acc{m}_{lo}", tag=f"bank{bank}")
             for a in range(PASSES):
@@ -116,7 +125,7 @@ def tile_list_tabhs_bias_kernel(tc, tab, w, b, wgo, offs, offs2, out):
                     start=(a == 0),
                     stop=(a == PASSES - 1),
                 )
-            nc.scalar.activation(y, acc[:], IDENTITY, bias=bias[:, m : m + 1])
+            nc.scalar.activation(y, acc[:], IDENTITY, bias=column)
 
         def put(m, lo, hi, y, weights):
             nc.vector.tensor_tensor(window[m % WINDOWS][:].indirect(place[:, lo // 16 : hi // 16]), y, weights, MULT)
@@ -134,15 +143,15 @@ def tile_list_tabhs_bias_kernel(tc, tab, w, b, wgo, offs, offs2, out):
         gather_words(1, 0, FIRST)
         gather_words(1, FIRST, S)
         y_first = keep.tile([P, FIRST], F32, name="y_first")
-        project(0, quantized, 0, FIRST, 0, y_first[:])
+        project(0, quantized, 0, FIRST, 0, y_first[:], bias_first[:])
         put(0, 0, FIRST, y_first[:], gate[:, 0:FIRST])
         following = quantize(1)
         load_weights(2)
         window.append(keep.tile([P, T], F32, name="window1", tag="grouped1", align_bytes=64))
         nc.gpsimd.memset(window[1][:], 0.0)
-        y_rest = keep.tile([P, S - FIRST], F32, name="y_rest", tag=slot[1][1], align_bytes=64)
-        project(0, quantized, FIRST, BANK, 1, y_rest[:, 0 : BANK - FIRST])
-        project(0, quantized, BANK, S, 2, y_rest[:, BANK - FIRST : S - FIRST])
+        y_rest = reuse.tile([P, S - FIRST], F32, name="y_rest", offset=start[1, 1])
+        project(0, quantized, FIRST, BANK, 1, y_rest[:, 0 : BANK - FIRST], bias[:, 0:1])
+        project(0, quantized, BANK, S, 2, y_rest[:, BANK - FIRST : S - FIRST], bias[:, 0:1])
         put(0, FIRST, S, y_rest[:], gate[:, FIRST:S])
         store(0)
         for m in range(1, BLOCKS):
@@ -151,10 +160,12 @@ def tile_list_tabhs_bias_kernel(tc, tab, w, b, wgo, offs, offs2, out):
                 following = quantize(m + 1)
                 if m + 2 < BLOCKS:
                     load_weights(m + 2)
-                y = keep.tile([P, S], F32, name=f"y{m}", tag=slot[m + 1][1], align_bytes=64)
+                    y = keep.tile([P, S], F32, name=f"y{m}", tag="grouped0", align_bytes=64)
+                else:
+                    y = reuse.tile([P, S], F32, name=f"y{m}", offset=start[3, 0])
             else:
                 y = keep.tile([P, S], F32, name=f"y{m}")
             for h in range(S // BANK):
-                project(m, quantized, h * BANK, (h + 1) * BANK, (1 + 2 * m + h) % 8, y[:, h * BANK : (h + 1) * BANK])
+                project(m, quantized, h * BANK, (h + 1) * BANK, (1 + 2 * m + h) % 8, y[:, h * BANK : (h + 1) * BANK], bias[:, m : m + 1])
             put(m, 0, S, y[:], gate[:])
             store(m)

@@ -32,15 +32,12 @@ def tile_list_tabhs_bias_kernel(tc, tab, w, b, wgo, offs, offs2, out):
         pick = keep.tile([P, S // 16], U16, name="pick")
         place = keep.tile([P, S // 16], U16, name="place")
 
-        scales = keep.tile([P, T], U8, name="scales", tag="picked0", align_bytes=64)
-        nc.vector.memset(scales[:].bitcast(I32), 0)
+        early = reuse.tile([P, 4 * T], U8, name="early", offset=4 * T)
+        scales = early[:, 0:T]
+        nc.vector.memset(scales.bitcast(I32), 0)
         scale_rows = tab[:, 512 * T :].rearrange("a (i c) -> i a c", i=16)
-        bias_rows = keep.tile([P, P], F32, name="bias_rows")
-        nc.vector.memset(bias_rows[:], 0.0)
         planes = keep.tile([P, PASSES * S], U8, name="planes", align_bytes=64)
         nc.vector.memset(planes[:].bitcast(I32), 0)
-        warm = keep.tile([P, 2], F32, name="warm")
-        nc.vector.memset(warm[:, 0:1], 0.0)
 
         words = [reuse.tile([P, T], I32, name="words0", offset=0), keep.tile([P, T], I32, name="words1", align_bytes=64)]
 
@@ -48,29 +45,28 @@ def tile_list_tabhs_bias_kernel(tc, tab, w, b, wgo, offs, offs2, out):
             nc.sync.dma_start(words[a][:], tab[a, 0 : 512 * T].rearrange("(p x) -> p x", p=P).bitcast(I32))
 
         w_rows = w.rearrange("(a p j) m -> a p j m", a=PASSES, j=4)
-        start = {(1, 0): 1024, (1, 1): 5120, (2, 0): 3072, (3, 0): 1024, (3, 1): 3072}
+        start = {(1, 0): 12288, (1, 1): 14336, (2, 0): 1024, (3, 0): 12288, (3, 1): 1024}
         raw = {}
 
-        def load_weights(m):
-            for a in range(PASSES):
+        def load_weights(m, passes=range(PASSES)):
+            for a in passes:
                 if (m, a) in start:
                     raw[m, a] = reuse.tile([P, 4, P], F32, name=f"raw{m}{a}", offset=start[m, a])
                 else:
                     raw[m, a] = keep.tile([P, 4, P], F32, name=f"raw{m}{a}", tag="grouped0" if m else f"raw{m}{a}", align_bytes=64)
                 nc.sync.dma_start(raw[m, a][:], w_rows[a][:, :, m * P : (m + 1) * P])
 
-        gate = keep.tile([P, S], F32, name="gate")
-
         nc.sync.dma_start(pick[:], offs)
+        load_weights(0, [0])
+        nc.sync.dma_start(early[0:P:4, 0:T].bitcast(I32), scale_rows.bitcast(I32))
         load_words(0)
-        nc.scalar.dma_start(scales[0:P:4, :].bitcast(I32), scale_rows.bitcast(I32))
-        nc.scalar.dma_start(bias_rows[0:BLOCKS, :], b.rearrange("(c p) -> c p", p=P))
-        nc.scalar.activation(warm[:, 1:2], warm[:, 0:1], IDENTITY)
+        load_weights(0, [1])
         nc.sync.dma_start(place[:], offs2)
-        load_weights(0)
         load_words(1)
-        nc.sync.dma_start(gate[:], wgo)
 
+        bias_rows = keep.tile([P, P], F32, name="bias_rows")
+        nc.gpsimd.memset(bias_rows[:], 0.0)
+        nc.scalar.dma_start(bias_rows[0:BLOCKS, :], b.rearrange("(c p) -> c p", p=P))
         identity = keep.tile([P, P], F32, name="identity")
         make_identity(nc, identity[:])
         turned = psum.tile([P, P], F32, name="turned", tag="bank7")
@@ -88,11 +84,15 @@ def tile_list_tabhs_bias_kernel(tc, tab, w, b, wgo, offs, offs2, out):
         def gather_words(a, lo, hi):
             nc.vector.tensor_copy(picked[a][:, lo:hi], words[a][:].bitcast(U32).indirect(pick[:, lo // 16 : hi // 16]))
 
-        nc.vector.tensor_copy(picked_scales[:], scales[:].indirect(pick[:]))
+        nc.vector.tensor_copy(picked_scales[:], scales.indirect(pick[:]))
         for q in range(4):
-            nc.scalar.dma_start(
+            nc.sync.dma_start(
                 planes[32 * q : 32 * q + 4, :].bitcast(I32), picked_scales[32 * q : 32 * q + 32 : 4, :].bitcast(I32)
             )
+        gate = reuse.tile([P, S], F32, name="gate", offset=4 * T)
+        nc.sync.dma_start(gate[:, 0:FIRST], wgo[:, 0:FIRST])
+        load_weights(1)
+        nc.sync.dma_start(gate[:, FIRST:S], wgo[:, FIRST:S])
         picked = [keep.tile([P, S], U32, name=f"picked{a}", tag=f"picked{a}", align_bytes=64) for a in range(PASSES)]
         gather_words(0, 0, S)
 
@@ -139,7 +139,6 @@ def tile_list_tabhs_bias_kernel(tc, tab, w, b, wgo, offs, offs2, out):
                 nc.scalar.dma_start(rows[:, T // 2 : T], window[m % WINDOWS][:, T // 2 : T])
 
         quantized = quantize(0)
-        load_weights(1)
         gather_words(1, 0, FIRST)
         gather_words(1, FIRST, S)
         y_first = keep.tile([P, FIRST], F32, name="y_first")
@@ -162,7 +161,7 @@ def tile_list_tabhs_bias_kernel(tc, tab, w, b, wgo, offs, offs2, out):
                     load_weights(m + 2)
                     y = keep.tile([P, S], F32, name=f"y{m}", tag="grouped0", align_bytes=64)
                 else:
-                    y = reuse.tile([P, S], F32, name=f"y{m}", offset=start[3, 0])
+                    y = reuse.tile([P, S], F32, name=f"y{m}", offset=start[3, 1])
             else:
                 y = keep.tile([P, S], F32, name=f"y{m}")
             for h in range(S // BANK):

@@ -77,7 +77,7 @@ def tile_list_tabhs_bias_kernel(tc, tab, w, b, wgo, offs, offs2, out):
         nc.scalar.copy(bias_first[:], turned[:, 0:1])
 
         window = [keep.tile([P, T], F32, name="window0")]
-        nc.gpsimd.memset(window[0][:], 0.0)
+        nc.vector.memset(window[0][:], 0.0)
 
         picked_scales = keep.tile([P, S], U8, name="picked_scales", align_bytes=64)
 

@@ -36,6 +36,8 @@ def tile_list_tabhs_bias_kernel(tc, tab, w, b, wgo, offs, offs2, out):
         scales = early[:, 0:T]
         nc.vector.memset(scales.bitcast(I32), 0)
         scale_rows = tab[:, 512 * T :].rearrange("a (i c) -> i a c", i=16)
+        bias_rows = keep.tile([P, P], F32, name="bias_rows")
+        nc.vector.memset(bias_rows[:], 0.0)
         planes = keep.tile([P, PASSES * S], U8, name="planes", align_bytes=64)
         nc.vector.memset(planes[:].bitcast(I32), 0)
 
@@ -64,11 +66,12 @@ def tile_list_tabhs_bias_kernel(tc, tab, w, b, wgo, offs, offs2, out):
         nc.sync.dma_start(place[:], offs2)
         load_words(1)
 
-        bias_rows = keep.tile([P, P], F32, name="bias_rows")
-        nc.gpsimd.memset(bias_rows[:], 0.0)
         nc.scalar.dma_start(bias_rows[0:BLOCKS, :], b.rearrange("(c p) -> c p", p=P))
+        window = [keep.tile([P, T], F32, name="window0")]
+        nc.vector.memset(window[0][:], 0.0)
         identity = keep.tile([P, P], F32, name="identity")
-        make_identity(nc, identity[:])
+        nc.vector.memset(identity[:], 0.0)
+        make_identity(nc, identity[:], nomemset=True)
         turned = psum.tile([P, P], F32, name="turned", tag="bank7")
         nc.tensor.transpose(turned[:], bias_rows[:], identity[:])
         bias = keep.tile([P, BLOCKS], F32, name="bias")
@@ -76,8 +79,6 @@ def tile_list_tabhs_bias_kernel(tc, tab, w, b, wgo, offs, offs2, out):
         bias_first = keep.tile([P, 1], F32, name="bias_first", tag="grouped1", align_bytes=64)
         nc.scalar.copy(bias_first[:], turned[:, 0:1])
 
-        window = [keep.tile([P, T], F32, name="window0")]
-        nc.vector.memset(window[0][:], 0.0)
 
         picked_scales = keep.tile([P, S], U8, name="picked_scales", align_bytes=64)
 

@@ -91,9 +91,9 @@ def tile_list_tabhs_bias_kernel(tc, tab, w, b, wgo, offs, offs2, out):
                 planes[32 * q : 32 * q + 4, :].bitcast(I32), picked_scales[32 * q : 32 * q + 32 : 4, :].bitcast(I32)
             )
         gate = reuse.tile([P, S], F32, name="gate", offset=4 * T)
-        nc.sync.dma_start(gate[:, 0:FIRST], wgo[:, 0:FIRST])
+        nc.sync.dma_start(gate[:, 0:BANK], wgo[:, 0:BANK])
         load_weights(1)
-        nc.sync.dma_start(gate[:, FIRST:S], wgo[:, FIRST:S])
+        nc.sync.dma_start(gate[:, BANK:S], wgo[:, BANK:S])
         picked = [keep.tile([P, S], U32, name=f"picked{a}", tag=f"picked{a}", align_bytes=64) for a in range(PASSES)]
         gather_words(0, 0, S)
 
@@ -104,10 +104,7 @@ def tile_list_tabhs_bias_kernel(tc, tab, w, b, wgo, offs, offs2, out):
                     grouped[:, a].rearrange("p (c i) j -> p c j i", i=4),
                     raw[m, a][:].rearrange("p j (c i) -> p c j i", i=4),
                 )
-            if m == 0:
-                codes = reuse.tile([P, PASSES * P], U32, name="codes0", offset=0, align_bytes=64)
-            else:
-                codes = keep.tile([P, PASSES * P], U32, name=f"codes{m}", align_bytes=64)
+            codes = keep.tile([P, PASSES * P], U32, name=f"codes{m}", align_bytes=64)
             plane = keep.tile([P, PASSES * P], U8, name=f"plane{m}", align_bytes=64)
             nc.vector.quantize_mx(out=codes[:].bitcast(FP8X4), scales=plane[:], in_=grouped[:].rearrange("p a c j -> p (a c j)"))
             return codes, plane
@@ -145,14 +142,16 @@ def tile_list_tabhs_bias_kernel(tc, tab, w, b, wgo, offs, offs2, out):
         y_first = keep.tile([P, FIRST], F32, name="y_first")
         project(0, quantized, 0, FIRST, 0, y_first[:], bias_first[:])
         put(0, 0, FIRST, y_first[:], gate[:, 0:FIRST])
+        y_second = keep.tile([P, BANK - FIRST], F32, name="y_second")
+        project(0, quantized, FIRST, BANK, 1, y_second[:], bias_first[:])
+        put(0, FIRST, BANK, y_second[:], gate[:, FIRST:BANK])
         following = quantize(1)
         load_weights(2)
         window.append(keep.tile([P, T], F32, name="window1", tag="grouped1", align_bytes=64))
         nc.gpsimd.memset(window[1][:], 0.0)
-        y_rest = reuse.tile([P, S - FIRST], F32, name="y_rest", offset=start[1, 1])
-        project(0, quantized, FIRST, BANK, 1, y_rest[:, 0 : BANK - FIRST], bias[:, 0:1])
-        project(0, quantized, BANK, S, 2, y_rest[:, BANK - FIRST : S - FIRST], bias[:, 0:1])
-        put(0, FIRST, S, y_rest[:], gate[:, FIRST:S])
+        y_rest = reuse.tile([P, S - BANK], F32, name="y_rest", offset=start[1, 1])
+        project(0, quantized, BANK, S, 2, y_rest[:], bias[:, 0:1])
+        put(0, BANK, S, y_rest[:], gate[:, BANK:S])
         store(0)
         for m in range(1, BLOCKS):
             quantized = following

@@ -39,7 +39,6 @@ def tile_list_tabhs_bias_kernel(tc, tab, w, b, wgo, offs, offs2, out):
         bias_rows = keep.tile([P, P], F32, name="bias_rows")
         nc.vector.memset(bias_rows[:], 0.0)
         planes = keep.tile([P, PASSES * S], U8, name="planes", align_bytes=64)
-        nc.vector.memset(planes[:].bitcast(I32), 0)
 
         words = [reuse.tile([P, T], I32, name="words0", offset=0), keep.tile([P, T], I32, name="words1", align_bytes=64)]
 
@@ -63,8 +62,8 @@ def tile_list_tabhs_bias_kernel(tc, tab, w, b, wgo, offs, offs2, out):
         nc.sync.dma_start(early[0:P:4, 0:T].bitcast(I32), scale_rows.bitcast(I32))
         load_words(0)
         load_weights(0, [1])
-        nc.sync.dma_start(place[:], offs2)
         load_words(1)
+        nc.sync.dma_start(place[:], offs2)
 
         nc.scalar.dma_start(bias_rows[0:BLOCKS, :], b.rearrange("(c p) -> c p", p=P))
         window = [keep.tile([P, T], F32, name="window0")]

@@ -17,7 +17,8 @@ P = 128
 K, M, T, S = 1024, 512, 2048, 1024
 PASSES = K // 512
 BANK = 512
-FIRST = 256
+FIRST = 384
+PIECE = 256
 BLOCKS = M // P
 WINDOWS = 2
 
@@ -136,21 +137,21 @@ def tile_list_tabhs_bias_kernel(tc, tab, w, b, wgo, offs, offs2, out):
                 nc.scalar.dma_start(rows[:, T // 2 : T], window[m % WINDOWS][:, T // 2 : T])
 
         quantized = quantize(0)
-        gather_words(1, 0, FIRST)
-        gather_words(1, FIRST, S)
+        gather_words(1, 0, PIECE)
+        gather_words(1, PIECE, BANK)
+        gather_words(1, BANK, S)
         y_first = keep.tile([P, FIRST], F32, name="y_first")
-        project(0, quantized, 0, FIRST, 0, y_first[:], bias_first[:])
+        project(0, quantized, 0, PIECE, 0, y_first[:, 0:PIECE], bias_first[:])
+        project(0, quantized, PIECE, FIRST, 1, y_first[:, PIECE:FIRST], bias_first[:])
         put(0, 0, FIRST, y_first[:], gate[:, 0:FIRST])
-        y_second = keep.tile([P, BANK - FIRST], F32, name="y_second")
-        project(0, quantized, FIRST, BANK, 1, y_second[:], bias_first[:])
-        put(0, FIRST, BANK, y_second[:], gate[:, FIRST:BANK])
         following = quantize(1)
         load_weights(2)
         window.append(keep.tile([P, T], F32, name="window1", tag="grouped1", align_bytes=64))
         nc.gpsimd.memset(window[1][:], 0.0)
-        y_rest = reuse.tile([P, S - BANK], F32, name="y_rest", offset=start[1, 1])
-        project(0, quantized, BANK, S, 2, y_rest[:], bias[:, 0:1])
-        put(0, BANK, S, y_rest[:], gate[:, BANK:S])
+        y_rest = reuse.tile([P, S - FIRST], F32, name="y_rest", offset=start[1, 1])
+        project(0, quantized, FIRST, BANK, 2, y_rest[:, 0 : BANK - FIRST], bias[:, 0:1])
+        project(0, quantized, BANK, S, 3, y_rest[:, BANK - FIRST : S - FIRST], bias[:, 0:1])
+        put(0, FIRST, S, y_rest[:], gate[:, FIRST:S])
         store(0)
         for m in range(1, BLOCKS):
             quantized = following
@@ -164,6 +165,6 @@ def tile_list_tabhs_bias_kernel(tc, tab, w, b, wgo, offs, offs2, out):
             else:
                 y = keep.tile([P, S], F32, name=f"y{m}")
             for h in range(S // BANK):
-                project(m, quantized, h * BANK, (h + 1) * BANK, (1 + 2 * m + h) % 8, y[:, h * BANK : (h + 1) * BANK], bias[:, m : m + 1])
+                project(m, quantized, h * BANK, (h + 1) * BANK, (2 + 2 * m + h) % 8, y[:, h * BANK : (h + 1) * BANK], bias[:, m : m + 1])
             put(m, 0, S, y[:], gate[:])
             store(m)

@@ -129,12 +129,7 @@ def tile_list_tabhs_bias_kernel(tc, tab, w, b, wgo, offs, offs2, out):
             nc.vector.tensor_tensor(window[m % WINDOWS][:].indirect(place[:, lo // 16 : hi // 16]), y, weights, MULT)
 
         def store(m):
-            rows = out[m * P : (m + 1) * P, :]
-            if m + 1 < BLOCKS:
-                nc.sync.dma_start(rows, window[m % WINDOWS][:])
-            else:
-                nc.sync.dma_start(rows[:, 0 : T // 2], window[m % WINDOWS][:, 0 : T // 2])
-                nc.scalar.dma_start(rows[:, T // 2 : T], window[m % WINDOWS][:, T // 2 : T])
+            nc.sync.dma_start(out[m * P : (m + 1) * P, :], window[m % WINDOWS][:])
 
         quantized = quantize(0)
         gather_words(1, 0, PIECE)

@@ -58,8 +58,8 @@ def tile_list_tabhs_bias_kernel(tc, tab, w, b, wgo, offs, offs2, out):
                     raw[m, a] = keep.tile([P, 4, P], F32, name=f"raw{m}{a}", tag="grouped0" if m else f"raw{m}{a}", align_bytes=64)
                 nc.sync.dma_start(raw[m, a][:], w_rows[a][:, :, m * P : (m + 1) * P])
 
-        nc.sync.dma_start(pick[:], offs)
         load_weights(0, [0])
+        nc.sync.dma_start(pick[:], offs)
         nc.sync.dma_start(early[0:P:4, 0:T].bitcast(I32), scale_rows.bitcast(I32))
         load_words(0)
         load_weights(0, [1])

@@ -56,7 +56,10 @@ def tile_list_tabhs_bias_kernel(tc, tab, w, b, wgo, offs, offs2, out):
                     raw[m, a] = reuse.tile([P, 4, P], F32, name=f"raw{m}{a}", offset=start[m, a])
                 else:
                     raw[m, a] = keep.tile([P, 4, P], F32, name=f"raw{m}{a}", tag="grouped0" if m else f"raw{m}{a}", align_bytes=64)
-                nc.sync.dma_start(raw[m, a][:], w_rows[a][:, :, m * P : (m + 1) * P])
+                parts = 2 if m >= 2 else 1
+                for h in range(parts):
+                    rows = slice(h * 4 // parts, (h + 1) * 4 // parts)
+                    nc.sync.dma_start(raw[m, a][:, rows], w_rows[a][:, rows, m * P : (m + 1) * P])
 
         load_weights(0, [0])
         nc.sync.dma_start(pick[:], offs)
@@ -86,14 +89,21 @@ def tile_list_tabhs_bias_kernel(tc, tab, w, b, wgo, offs, offs2, out):
             nc.vector.tensor_copy(picked[a][:, lo:hi], words[a][:].bitcast(U32).indirect(pick[:, lo // 16 : hi // 16]))
 
         nc.vector.tensor_copy(picked_scales[:], scales.indirect(pick[:]))
-        for q in range(4):
-            nc.sync.dma_start(
-                planes[32 * q : 32 * q + 4, :].bitcast(I32), picked_scales[32 * q : 32 * q + 32 : 4, :].bitcast(I32)
-            )
+
+        def move_scales(lo, hi):
+            for q in range(4):
+                nc.sync.dma_start(
+                    planes[32 * q : 32 * q + 4, :].rearrange("p (a s) -> p a s", a=PASSES)[:, :, lo:hi].bitcast(I32),
+                    picked_scales[32 * q : 32 * q + 32 : 4, lo:hi].bitcast(I32),
+                )
+
+        move_scales(0, FIRST)
         gate = reuse.tile([P, S], F32, name="gate", offset=4 * T)
-        nc.sync.dma_start(gate[:, 0:BANK], wgo[:, 0:BANK])
-        load_weights(1)
-        nc.sync.dma_start(gate[:, BANK:S], wgo[:, BANK:S])
+        nc.sync.dma_start(gate[:, 0:FIRST], wgo[:, 0:FIRST])
+        load_weights(1, [0])
+        move_scales(FIRST, S)
+        load_weights(1, [1])
+        nc.sync.dma_start(gate[:, FIRST:S], wgo[:, FIRST:S])
         picked = [keep.tile([P, S], U32, name=f"picked{a}", tag=f"picked{a}", align_bytes=64) for a in range(PASSES)]
         gather_words(0, 0, S)
 

@@ -56,7 +56,7 @@ def tile_list_tabhs_bias_kernel(tc, tab, w, b, wgo, offs, offs2, out):
                     raw[m, a] = reuse.tile([P, 4, P], F32, name=f"raw{m}{a}", offset=start[m, a])
                 else:
                     raw[m, a] = keep.tile([P, 4, P], F32, name=f"raw{m}{a}", tag="grouped0" if m else f"raw{m}{a}", align_bytes=64)
-                parts = 2 if m >= 2 else 1
+                parts = 2 if (m, a) == (3, 1) else 1
                 for h in range(parts):
                     rows = slice(h * 4 // parts, (h + 1) * 4 // parts)
                     nc.sync.dma_start(raw[m, a][:, rows], w_rows[a][:, rows, m * P : (m + 1) * P])
@@ -139,7 +139,10 @@ def tile_list_tabhs_bias_kernel(tc, tab, w, b, wgo, offs, offs2, out):
             nc.vector.tensor_tensor(window[m % WINDOWS][:].indirect(place[:, lo // 16 : hi // 16]), y, weights, MULT)
 
         def store(m):
-            nc.sync.dma_start(out[m * P : (m + 1) * P, :], window[m % WINDOWS][:])
+            parts = 4 if m == BLOCKS - 2 else 1
+            for h in range(parts):
+                cols = slice(h * T // parts, (h + 1) * T // parts)
+                nc.sync.dma_start(out[m * P : (m + 1) * P, cols], window[m % WINDOWS][:, cols])
 
         quantized = quantize(0)
         gather_words(1, 0, PIECE)

@@ -16,11 +16,21 @@ IDENTITY = mybir.ActivationFunctionType.Identity
 P = 128
 K, M, T, S = 1024, 512, 2048, 1024
 PASSES = K // 512
-BANK = 512
-FIRST = 384
-PIECE = 256
 BLOCKS = M // P
+BANK = 512
+BANKS = 8
 WINDOWS = 2
+GROUP = 16
+
+PIECE = 256
+FIRST = 384
+THIRD_STORE_WIDTH = 416
+
+EARLY = 4 * T
+RAW_BYTES = 4 * P * 4
+SLOT_A = EARLY + 4 * S
+SLOT_B = SLOT_A + RAW_BYTES
+SLOT_C = 1024
 
 
 def tile_list_tabhs_bias_kernel(tc, tab, w, b, wgo, offs, offs2, out):
@@ -30,10 +40,10 @@ def tile_list_tabhs_bias_kernel(tc, tab, w, b, wgo, offs, offs2, out):
         tc.tile_pool(name="reuse", bufs=1) as reuse,
         tc.psum_pool(name="psum", bufs=1) as psum,
     ):
-        pick = keep.tile([P, S // 16], U16, name="pick")
-        place = keep.tile([P, S // 16], U16, name="place")
+        pick = keep.tile([P, S // GROUP], U16, name="pick")
+        place = keep.tile([P, S // GROUP], U16, name="place")
 
-        early = reuse.tile([P, 4 * T], U8, name="early", offset=4 * T)
+        early = reuse.tile([P, 4 * T], U8, name="early", offset=EARLY)
         scales = early[:, 0:T]
         nc.vector.memset(scales.bitcast(I32), 0)
         scale_rows = tab[:, 512 * T :].rearrange("a (i c) -> i a c", i=16)
@@ -46,20 +56,17 @@ def tile_list_tabhs_bias_kernel(tc, tab, w, b, wgo, offs, offs2, out):
         def load_words(a):
             nc.sync.dma_start(words[a][:], tab[a, 0 : 512 * T].rearrange("(p x) -> p x", p=P).bitcast(I32))
 
-        w_rows = w.rearrange("(a p j) m -> a p j m", a=PASSES, j=4)
-        start = {(1, 0): 12288, (1, 1): 14336, (2, 0): 1024, (3, 0): 12288, (3, 1): 1024}
+        w_rows = w.rearrange("(a p t) m -> a p t m", a=PASSES, t=4)
+        slot = {(1, 0): SLOT_A, (1, 1): SLOT_B, (2, 0): SLOT_C, (3, 0): SLOT_A, (3, 1): SLOT_C}
         raw = {}
 
         def load_weights(m, passes=range(PASSES)):
             for a in passes:
-                if (m, a) in start:
-                    raw[m, a] = reuse.tile([P, 4, P], F32, name=f"raw{m}{a}", offset=start[m, a])
+                if (m, a) in slot:
+                    raw[m, a] = reuse.tile([P, 4, P], F32, name=f"raw{m}{a}", offset=slot[m, a])
                 else:
                     raw[m, a] = keep.tile([P, 4, P], F32, name=f"raw{m}{a}", tag="grouped0" if m else f"raw{m}{a}", align_bytes=64)
-                parts = 2 if (m, a) == (3, 1) else 1
-                for h in range(parts):
-                    rows = slice(h * 4 // parts, (h + 1) * 4 // parts)
-                    nc.sync.dma_start(raw[m, a][:, rows], w_rows[a][:, rows, m * P : (m + 1) * P])
+                nc.sync.dma_start(raw[m, a][:], w_rows[a][:, :, m * P : (m + 1) * P])
 
         load_weights(0, [0])
         nc.sync.dma_start(pick[:], offs)
@@ -67,27 +74,21 @@ def tile_list_tabhs_bias_kernel(tc, tab, w, b, wgo, offs, offs2, out):
         load_words(0)
         load_weights(0, [1])
         load_words(1)
-        nc.sync.dma_start(place[:], offs2)
 
         nc.scalar.dma_start(bias_rows[0:BLOCKS, :], b.rearrange("(c p) -> c p", p=P))
         window = [keep.tile([P, T], F32, name="window0")]
         nc.vector.memset(window[0][:], 0.0)
-        identity = keep.tile([P, P], F32, name="identity")
+        identity = keep.tile([P, P], F32, name="identity", tag="identity")
         nc.vector.memset(identity[:], 0.0)
         make_identity(nc, identity[:], nomemset=True)
-        turned = psum.tile([P, P], F32, name="turned", tag="bank7")
+        turned = psum.tile([P, P], F32, name="turned", tag=f"bank{BANKS - 1}")
         nc.tensor.transpose(turned[:], bias_rows[:], identity[:])
         bias = keep.tile([P, BLOCKS], F32, name="bias")
         nc.scalar.copy(bias[:], turned[:, 0:BLOCKS])
         bias_first = keep.tile([P, 1], F32, name="bias_first", tag="grouped1", align_bytes=64)
         nc.scalar.copy(bias_first[:], turned[:, 0:1])
 
-
         picked_scales = keep.tile([P, S], U8, name="picked_scales", align_bytes=64)
-
-        def gather_words(a, lo, hi):
-            nc.vector.tensor_copy(picked[a][:, lo:hi], words[a][:].bitcast(U32).indirect(pick[:, lo // 16 : hi // 16]))
-
         nc.vector.tensor_copy(picked_scales[:], scales.indirect(pick[:]))
 
         def move_scales(lo, hi):
@@ -98,25 +99,29 @@ def tile_list_tabhs_bias_kernel(tc, tab, w, b, wgo, offs, offs2, out):
                 )
 
         move_scales(0, FIRST)
-        gate = reuse.tile([P, S], F32, name="gate", offset=4 * T)
+        nc.sync.dma_start(place[:], offs2)
+        gate = reuse.tile([P, S], F32, name="gate", offset=EARLY)
         nc.sync.dma_start(gate[:, 0:FIRST], wgo[:, 0:FIRST])
         load_weights(1, [0])
         move_scales(FIRST, S)
         load_weights(1, [1])
         nc.sync.dma_start(gate[:, FIRST:S], wgo[:, FIRST:S])
+
         picked = [keep.tile([P, S], U32, name=f"picked{a}", tag=f"picked{a}", align_bytes=64) for a in range(PASSES)]
-        gather_words(0, 0, S)
+
+        def gather_words(a, lo, hi):
+            nc.vector.tensor_copy(picked[a][:, lo:hi], words[a][:].bitcast(U32).indirect(pick[:, lo // GROUP : hi // GROUP]))
 
         def quantize(m):
             grouped = keep.tile([P, PASSES, P, 4], BF16, name=f"grouped{m}", tag=f"grouped{m}", align_bytes=64)
             for a in range(PASSES):
                 nc.scalar.copy(
-                    grouped[:, a].rearrange("p (c i) j -> p c j i", i=4),
-                    raw[m, a][:].rearrange("p j (c i) -> p c j i", i=4),
+                    grouped[:, a].rearrange("p (c i) t -> p c t i", i=4),
+                    raw[m, a][:].rearrange("p t (c i) -> p c t i", i=4),
                 )
             codes = keep.tile([P, PASSES * P], U32, name=f"codes{m}", align_bytes=64)
             plane = keep.tile([P, PASSES * P], U8, name=f"plane{m}", align_bytes=64)
-            nc.vector.quantize_mx(out=codes[:].bitcast(FP8X4), scales=plane[:], in_=grouped[:].rearrange("p a c j -> p (a c j)"))
+            nc.vector.quantize_mx(out=codes[:].bitcast(FP8X4), scales=plane[:], in_=grouped[:].rearrange("p a c t -> p (a c t)"))
             return codes, plane
 
         def project(m, quantized, lo, hi, bank, y, column):
@@ -135,32 +140,36 @@ def tile_list_tabhs_bias_kernel(tc, tab, w, b, wgo, offs, offs2, out):
                 )
             nc.scalar.activation(y, acc[:], IDENTITY, bias=column)
 
-        def put(m, lo, hi, y, weights):
-            nc.vector.tensor_tensor(window[m % WINDOWS][:].indirect(place[:, lo // 16 : hi // 16]), y, weights, MULT)
+        def put(m, lo, hi, y):
+            target = window[m % WINDOWS][:].indirect(place[:, lo // GROUP : hi // GROUP])
+            nc.vector.tensor_tensor(target, y, gate[:, lo:hi], MULT)
 
         def store(m):
-            parts = 4 if m == BLOCKS - 2 else 1
-            for h in range(parts):
-                cols = slice(h * T // parts, (h + 1) * T // parts)
+            width = THIRD_STORE_WIDTH if m == BLOCKS - 2 else T
+            for lo in range(0, T, width):
+                cols = slice(lo, min(lo + width, T))
                 nc.sync.dma_start(out[m * P : (m + 1) * P, cols], window[m % WINDOWS][:, cols])
 
+        gather_words(0, 0, S)
         quantized = quantize(0)
         gather_words(1, 0, PIECE)
         gather_words(1, PIECE, BANK)
         gather_words(1, BANK, S)
+
         y_first = keep.tile([P, FIRST], F32, name="y_first")
         project(0, quantized, 0, PIECE, 0, y_first[:, 0:PIECE], bias_first[:])
         project(0, quantized, PIECE, FIRST, 1, y_first[:, PIECE:FIRST], bias_first[:])
-        put(0, 0, FIRST, y_first[:], gate[:, 0:FIRST])
+        put(0, 0, FIRST, y_first[:])
         following = quantize(1)
         load_weights(2)
-        window.append(keep.tile([P, T], F32, name="window1", tag="grouped1", align_bytes=64))
+        window.append(keep.tile([P, T], F32, name="window1", tag="identity"))
         nc.gpsimd.memset(window[1][:], 0.0)
-        y_rest = reuse.tile([P, S - FIRST], F32, name="y_rest", offset=start[1, 1])
+        y_rest = reuse.tile([P, S - FIRST], F32, name="y_rest", offset=slot[1, 1])
         project(0, quantized, FIRST, BANK, 2, y_rest[:, 0 : BANK - FIRST], bias[:, 0:1])
         project(0, quantized, BANK, S, 3, y_rest[:, BANK - FIRST : S - FIRST], bias[:, 0:1])
-        put(0, FIRST, S, y_rest[:], gate[:, FIRST:S])
+        put(0, FIRST, S, y_rest[:])
         store(0)
+
         for m in range(1, BLOCKS):
             quantized = following
             if m + 1 < BLOCKS:
@@ -169,10 +178,11 @@ def tile_list_tabhs_bias_kernel(tc, tab, w, b, wgo, offs, offs2, out):
                     load_weights(m + 2)
                     y = keep.tile([P, S], F32, name=f"y{m}", tag="grouped0", align_bytes=64)
                 else:
-                    y = reuse.tile([P, S], F32, name=f"y{m}", offset=start[3, 1])
+                    y = reuse.tile([P, S], F32, name=f"y{m}", offset=slot[m + 1, 1])
             else:
                 y = keep.tile([P, S], F32, name=f"y{m}")
             for h in range(S // BANK):
-                project(m, quantized, h * BANK, (h + 1) * BANK, (2 + 2 * m + h) % 8, y[:, h * BANK : (h + 1) * BANK], bias[:, m : m + 1])
-            put(m, 0, S, y[:], gate[:])
+                bank = (2 + 2 * m + h) % BANKS
+                project(m, quantized, h * BANK, (h + 1) * BANK, bank, y[:, h * BANK : (h + 1) * BANK], bias[:, m : m + 1])
+            put(m, 0, S, y[:])
             store(m)

@@ -70,7 +70,7 @@ def tile_list_tabhs_bias_kernel(tc, tab, w, b, wgo, offs, offs2, out):
 
         load_weights(0, [0])
         nc.sync.dma_start(pick[:], offs)
-        nc.sync.dma_start(early[0:P:4, 0:T].bitcast(I32), scale_rows.bitcast(I32))
+        nc.sync.dma_start(early[32:96:2, 0:T].bitcast(I32), scale_rows.bitcast(I32))
         load_words(0)
         load_weights(0, [1])
         load_words(1)
@@ -95,7 +95,7 @@ def tile_list_tabhs_bias_kernel(tc, tab, w, b, wgo, offs, offs2, out):
             for q in range(4):
                 nc.sync.dma_start(
                     planes[32 * q : 32 * q + 4, :].rearrange("p (a s) -> p a s", a=PASSES)[:, :, lo:hi].bitcast(I32),
-                    picked_scales[32 * q : 32 * q + 32 : 4, lo:hi].bitcast(I32),
+                    picked_scales[32 + 16 * q : 48 + 16 * q : 2, lo:hi].bitcast(I32),
                 )
 
         move_scales(0, FIRST)

import concourse.mybir as mybir
from concourse.masks import make_identity

FLOPS = 2 * 1024 * 512 * 1024

F32 = mybir.dt.float32
BF16 = mybir.dt.bfloat16
I32 = mybir.dt.int32
U32 = mybir.dt.uint32
U16 = mybir.dt.uint16
U8 = mybir.dt.uint8
FP8X4 = mybir.dt.float8_e4m3fn_x4
MULT = mybir.AluOpType.mult
IDENTITY = mybir.ActivationFunctionType.Identity

P = 128
K, M, T, S = 1024, 512, 2048, 1024
PASSES = K // 512
BLOCKS = M // P
BANK = 512
BANKS = 8
WINDOWS = 2
GROUP = 16

PIECE = 256
FIRST = 384
THIRD_STORE_WIDTH = 416

EARLY = 4 * T
RAW_BYTES = 4 * P * 4
SLOT_A = EARLY + 4 * S
SLOT_B = SLOT_A + RAW_BYTES
SLOT_C = 1024


def tile_list_tabhs_bias_kernel(tc, tab, w, b, wgo, offs, offs2, out):
    nc = tc.nc
    with (
        tc.tile_pool(name="keep", bufs=1) as keep,
        tc.tile_pool(name="reuse", bufs=1) as reuse,
        tc.psum_pool(name="psum", bufs=1) as psum,
    ):
        pick = keep.tile([P, S // GROUP], U16, name="pick")
        place = keep.tile([P, S // GROUP], U16, name="place")

        early = reuse.tile([P, 4 * T], U8, name="early", offset=EARLY)
        scales = early[:, 0:T]
        nc.vector.memset(scales.bitcast(I32), 0)
        scale_rows = tab[:, 512 * T :].rearrange("a (i c) -> i a c", i=16)
        bias_rows = keep.tile([P, P], F32, name="bias_rows")
        nc.vector.memset(bias_rows[:], 0.0)
        planes = keep.tile([P, PASSES * S], U8, name="planes", align_bytes=64)

        words = [reuse.tile([P, T], I32, name="words0", offset=0), keep.tile([P, T], I32, name="words1", align_bytes=64)]

        def load_words(a):
            nc.sync.dma_start(words[a][:], tab[a, 0 : 512 * T].rearrange("(p x) -> p x", p=P).bitcast(I32))

        w_rows = w.rearrange("(a p t) m -> a p t m", a=PASSES, t=4)
        slot = {(1, 0): SLOT_A, (1, 1): SLOT_B, (2, 0): SLOT_C, (3, 0): SLOT_A, (3, 1): SLOT_C}
        raw = {}

        def load_weights(m, passes=range(PASSES)):
            for a in passes:
                if (m, a) in slot:
                    raw[m, a] = reuse.tile([P, 4, P], F32, name=f"raw{m}{a}", offset=slot[m, a])
                else:
                    raw[m, a] = keep.tile([P, 4, P], F32, name=f"raw{m}{a}", tag="grouped0" if m else f"raw{m}{a}", align_bytes=64)
                nc.sync.dma_start(raw[m, a][:], w_rows[a][:, :, m * P : (m + 1) * P])

        load_weights(0, [0])
        nc.sync.dma_start(pick[:], offs)
        nc.sync.dma_start(early[32:96:2, 0:T].bitcast(I32), scale_rows.bitcast(I32))
        load_words(0)
        load_weights(0, [1])
        load_words(1)

        nc.scalar.dma_start(bias_rows[0:BLOCKS, :], b.rearrange("(c p) -> c p", p=P))
        window = [keep.tile([P, T], F32, name="window0")]
        nc.vector.memset(window[0][:], 0.0)
        identity = keep.tile([P, P], F32, name="identity", tag="identity")
        nc.vector.memset(identity[:], 0.0)
        make_identity(nc, identity[:], nomemset=True)
        turned = psum.tile([P, P], F32, name="turned", tag=f"bank{BANKS - 1}")
        nc.tensor.transpose(turned[:], bias_rows[:], identity[:])
        bias = keep.tile([P, BLOCKS], F32, name="bias")
        nc.scalar.copy(bias[:], turned[:, 0:BLOCKS])
        bias_first = keep.tile([P, 1], F32, name="bias_first", tag="grouped1", align_bytes=64)
        nc.scalar.copy(bias_first[:], turned[:, 0:1])

        picked_scales = keep.tile([P, S], U8, name="picked_scales", align_bytes=64)
        nc.vector.tensor_copy(picked_scales[:], scales.indirect(pick[:]))

        def move_scales(lo, hi):
            for q in range(4):
                nc.sync.dma_start(
                    planes[32 * q : 32 * q + 4, :].rearrange("p (a s) -> p a s", a=PASSES)[:, :, lo:hi].bitcast(I32),
                    picked_scales[32 + 16 * q : 48 + 16 * q : 2, lo:hi].bitcast(I32),
                )

        move_scales(0, FIRST)
        nc.sync.dma_start(place[:], offs2)
        gate = reuse.tile([P, S], F32, name="gate", offset=EARLY)
        nc.sync.dma_start(gate[:, 0:FIRST], wgo[:, 0:FIRST])
        load_weights(1, [0])
        move_scales(FIRST, S)
        load_weights(1, [1])
        nc.sync.dma_start(gate[:, FIRST:S], wgo[:, FIRST:S])

        picked = [keep.tile([P, S], U32, name=f"picked{a}", tag=f"picked{a}", align_bytes=64) for a in range(PASSES)]

        def gather_words(a, lo, hi):
            nc.vector.tensor_copy(picked[a][:, lo:hi], words[a][:].bitcast(U32).indirect(pick[:, lo // GROUP : hi // GROUP]))

        def quantize(m):
            grouped = keep.tile([P, PASSES, P, 4], BF16, name=f"grouped{m}", tag=f"grouped{m}", align_bytes=64)
            for a in range(PASSES):
                nc.scalar.copy(
                    grouped[:, a].rearrange("p (c i) t -> p c t i", i=4),
                    raw[m, a][:].rearrange("p t (c i) -> p c t i", i=4),
                )
            codes = keep.tile([P, PASSES * P], U32, name=f"codes{m}", align_bytes=64)
            plane = keep.tile([P, PASSES * P], U8, name=f"plane{m}", align_bytes=64)
            nc.vector.quantize_mx(out=codes[:].bitcast(FP8X4), scales=plane[:], in_=grouped[:].rearrange("p a c t -> p (a c t)"))
            return codes, plane

        def project(m, quantized, lo, hi, bank, y, column):
            codes, plane = quantized
            acc = psum.tile([P, hi - lo], F32, name=f"acc{m}_{lo}", tag=f"bank{bank}")
            for a in range(PASSES):
                c0 = a * P
                nc.tensor.matmul_mx(
                    out=acc[:],
                    lhsT=codes[:, c0 : c0 + P].bitcast(FP8X4),
                    lhsT_scale=plane[:, c0 : c0 + P],
                    rhs=picked[a][:, lo:hi].bitcast(FP8X4),
                    rhs_scale=planes[:, a * S + lo : a * S + hi],
                    start=(a == 0),
                    stop=(a == PASSES - 1),
                )
            nc.scalar.activation(y, acc[:], IDENTITY, bias=column)

        def put(m, lo, hi, y):
            target = window[m % WINDOWS][:].indirect(place[:, lo // GROUP : hi // GROUP])
            nc.vector.tensor_tensor(target, y, gate[:, lo:hi], MULT)

        def store(m):
            width = THIRD_STORE_WIDTH if m == BLOCKS - 2 else T
            for lo in range(0, T, width):
                cols = slice(lo, min(lo + width, T))
                nc.sync.dma_start(out[m * P : (m + 1) * P, cols], window[m % WINDOWS][:, cols])

        gather_words(0, 0, S)
        quantized = quantize(0)
        gather_words(1, 0, PIECE)
        gather_words(1, PIECE, BANK)
        gather_words(1, BANK, S)

        y_first = keep.tile([P, FIRST], F32, name="y_first")
        project(0, quantized, 0, PIECE, 0, y_first[:, 0:PIECE], bias_first[:])
        project(0, quantized, PIECE, FIRST, 1, y_first[:, PIECE:FIRST], bias_first[:])
        put(0, 0, FIRST, y_first[:])
        following = quantize(1)
        load_weights(2)
        window.append(keep.tile([P, T], F32, name="window1", tag="identity"))
        nc.gpsimd.memset(window[1][:], 0.0)
        y_rest = reuse.tile([P, S - FIRST], F32, name="y_rest", offset=slot[1, 1])
        project(0, quantized, FIRST, BANK, 2, y_rest[:, 0 : BANK - FIRST], bias[:, 0:1])
        project(0, quantized, BANK, S, 3, y_rest[:, BANK - FIRST : S - FIRST], bias[:, 0:1])
        put(0, FIRST, S, y_rest[:])
        store(0)

        for m in range(1, BLOCKS):
            quantized = following
            if m + 1 < BLOCKS:
                following = quantize(m + 1)
                if m + 2 < BLOCKS:
                    load_weights(m + 2)
                    y = keep.tile([P, S], F32, name=f"y{m}", tag="grouped0", align_bytes=64)
                else:
                    y = reuse.tile([P, S], F32, name=f"y{m}", offset=slot[m + 1, 1])
            else:
                y = keep.tile([P, S], F32, name=f"y{m}")
            for h in range(S // BANK):
                bank = (2 + 2 * m + h) % BANKS
                project(m, quantized, h * BANK, (h + 1) * BANK, bank, y[:, h * BANK : (h + 1) * BANK], bias[:, m : m + 1])
            put(m, 0, S, y[:])
            store(m)
